import numpy as np
import ml_dtypes


def mxq(x, axis, fmt="e4m3"):
    dtype, down = {"e4m3": (ml_dtypes.float8_e4m3fn, 7), "e5m2": (ml_dtypes.float8_e5m2, 14)}[fmt]
    v = np.moveaxis(np.asarray(x, np.float32).astype(ml_dtypes.bfloat16).astype(np.float64), axis, -1)
    blocks = v.reshape(v.shape[:-1] + (-1, 32))
    amax = np.abs(blocks).max(-1, keepdims=True)
    byte = np.maximum(np.where(amax > 0, np.frexp(amax)[1] - 1 + 127, 0) - down, 1)
    scale = np.exp2(byte - 127.0)
    codes = (blocks / scale).astype(np.float32).astype(dtype).astype(np.float64)
    return np.moveaxis((codes * scale).reshape(v.shape), -1, axis)


WIDE = False


def mx_kscale(k):
    if not WIDE:
        return np.ones(k)
    levels = np.array([10, -10, 5, -5, 0])
    if k % 512:
        return np.exp2(np.random.permutation(np.resize(levels, k // 32))).repeat(32)
    a = np.empty((k // 512, 16))
    for p in range(k // 512):
        a[p, :8] = np.random.permutation(np.resize(levels, 8))
        for g in range(8):
            far = levels[np.abs(levels - a[p, g]) >= 10]
            a[p, g + 8] = far[np.random.randint(len(far))]
    return np.exp2(a.ravel()).repeat(32)


def f64(x):
    return np.asarray(x).astype(np.float64)


def striped(idx):
    return np.tile(idx.reshape(-1, 16).T, (8, 1)).astype(np.uint16)


def unstriped(offs):
    return offs[:16].T.reshape(-1).astype(np.int64)


def striped8(idx):
    return np.concatenate([x.reshape(-1, 16).T for x in idx]).astype(np.uint16)


def runs(offs, k):
    lists = np.stack([offs[16 * r : 16 * r + 16].T.reshape(-1) for r in range(8)]).astype(np.int64)
    return lists[np.arange(k) % 512 // 64]


def pack_weight(w):
    k, n = w.shape
    w = f64(np.asarray(w, np.float32).astype(ml_dtypes.bfloat16)).reshape(k // 32, 32, n)
    amax = np.abs(w).max(1)
    byte = np.clip(np.where(amax > 0, np.frexp(amax)[1] - 1 + 127 - 7, 1), 1, 254)
    scaled = (w * np.exp2(127.0 - byte)[:, None, :]).reshape(k, n).astype(np.float32)
    words = np.ascontiguousarray(scaled.reshape(k // 512, 128, 4, n).transpose(0, 1, 3, 2)).astype(ml_dtypes.float8_e4m3fn).view(np.uint8)
    return words, np.ascontiguousarray(byte.astype(np.uint8).reshape(k // 512, 16, n))


def unpack_weight(words, scales):
    g, p, n, _ = words.shape
    vals = np.ascontiguousarray(words).view(ml_dtypes.float8_e4m3fn).astype(np.float64) * np.repeat(np.exp2(scales.astype(np.float64) - 127.0), 8, axis=1)[..., None]
    return vals.transpose(0, 1, 3, 2).reshape(g * 512, n)


def sigmoid(v):
    return 1.0 / (1.0 + np.exp(-np.maximum(v, -700.0)))


K, T, S, N, H = 512, 2048, 512, 512, 512


def setup_inputs():
    n = np.random.standard_normal
    s = mx_kscale(K)[:, None]
    u = mx_kscale(S)
    packed_xT = pack_weight(n((K, T)) * s)
    return {
        "x_words": packed_xT[0],
        "x_scales": packed_xT[1],
        "wa": (n((K, H)) / np.sqrt(K) / s).astype(np.float32),
        "gt": (np.random.uniform(0.5, 1.5, (S, 1)) * u[:, None]).astype(np.float32),
        "w1": (n((S, H)) / np.sqrt(S) / u[:, None]).astype(np.float32),
        "gp": (np.random.uniform(0.5, 1.5, (H, 1)) * u[:, None]).astype(np.float32),
        "res": (1.5 * n((N, H))).astype(np.float32),
        "w2": (n((H, N)) / np.sqrt(H) / u[:, None]).astype(np.float32),
        "offs": striped(np.random.permutation(T)[:S]),
        "n1": striped8(np.stack([np.random.permutation(H) for _ in range(8)])),
        "n2": striped8(np.stack([np.random.permutation(H) for _ in range(8)])),
        "n3": striped8(np.stack([np.random.permutation(H) for _ in range(8)])),
        "n4": striped8(np.stack([np.random.permutation(H) for _ in range(8)])),
        "n5": striped8(np.stack([np.random.permutation(H) for _ in range(8)])),
    }


def reference(x_words, x_scales, wa, gt, w1, gp, res, w2, offs, n1, n2, n3, n4, n5):
    xq = unpack_weight(x_words, x_scales)[:, unstriped(offs)]
    y = xq.T @ mxq(f64(wa), 0, "e4m3")
    st = y - (y[np.arange(S)[:, None], runs(n1, S)])
    z = f64(gt) * (np.maximum(st, st[np.arange(S)[:, None], runs(n2, S)]))
    h = mxq(f64(w1), 0, "e4m3").T @ mxq(z, 0, "e4m3")
    pa = h[np.arange(H)[:, None], runs(n3, H)]
    z2 = f64(gp) * (pa + (sigmoid(h[np.arange(H)[:, None], runs(n4, H)])) * (h[np.arange(H)[:, None], runs(n5, H)] - pa))
    return f64(res) + (mxq(f64(w2), 0, "e4m3").T @ mxq(z2, 0, "e4m3"))

@@ -1,0 +1,240 @@
+from contextlib import ExitStack
+
+import concourse.mybir as mybir
+
+K, T, S, H, N = 512, 2048, 512, 512, 512
+FLOPS = 2 * (K * S * H + S * H * H + H * N * H)
+
+F32 = mybir.dt.float32
+BF16 = mybir.dt.bfloat16
+I32 = mybir.dt.int32
+U32 = mybir.dt.uint32
+U16 = mybir.dt.uint16
+U8 = mybir.dt.uint8
+FP8X4 = mybir.dt.float8_e4m3fn_x4
+ALU = mybir.AluOpType
+ACT = mybir.ActivationFunctionType
+
+P = 128
+PACK = 4
+PER_COL = 16
+HALF = H // 2
+FIRST_HOP_CHUNKS = (256, 128, 128)
+SECOND_HOP_CHUNKS = (128, 128, 128, 128)
+FUSED_SECOND = 3
+FINITE = 3.0e38
+
+
+def chunks(widths):
+    start = 0
+    spans = []
+    for width in widths:
+        spans.append((start, width))
+        start = start + width
+    return spans
+
+
+def entries(lists, start, width):
+    return lists[:, start // PER_COL : (start + width) // PER_COL]
+
+
+def by_lines_src(ap):
+    return ap.rearrange("p t (c i) -> p c t i", i=4)
+
+
+def by_lines_dst(ap):
+    return ap.rearrange("p (c i) t -> p c t i", i=4)
+
+
+def quantize(nc, codes, scales, grouped):
+    nc.vector.quantize_mx(out=codes.bitcast(FP8X4), scales=scales, in_=grouped)
+
+
+def product(nc, acc, lhs_codes, lhs_scales, rhs_codes, rhs_scales):
+    nc.tensor.matmul_mx(
+        out=acc,
+        lhsT=lhs_codes.bitcast(FP8X4),
+        lhsT_scale=lhs_scales,
+        rhs=rhs_codes.bitcast(FP8X4),
+        rhs_scale=rhs_scales,
+        start=True,
+        stop=True,
+    )
+
+
+def tile_picked_tok2hopmxlerp_none_p_kernel(
+    tc, x_words, x_scales, wa, gt, w1, gp, res, w2, offs, n1, n2, n3, n4, n5, out
+):
+    nc = tc.nc
+    with ExitStack() as ctx:
+        keep = ctx.enter_context(tc.tile_pool(name="keep", bufs=1))
+        psum = ctx.enter_context(tc.psum_pool(name="psum", bufs=1))
+
+        def sbuf(name, shape, dtype, tag=None):
+            return keep.tile(shape, dtype, name=name, tag=tag or name, align_bytes=64)
+
+        def load_list(name, lists):
+            tile = keep.tile([P, S // PER_COL], U16, name=name)
+            nc.sync.dma_start(tile[:], lists)
+            return tile
+
+        def load_rows(name, rows):
+            tile = sbuf(name, [P, PACK, rows.shape[1]], F32)
+            nc.sync.dma_start(tile[:], rows.rearrange("(p t) c -> p t c", t=PACK))
+            return tile
+
+        offs_sb = load_list("offs_sb", offs)
+        n1_sb = load_list("n1_sb", n1)
+        n2_sb = load_list("n2_sb", n2)
+        gt_sb = load_rows("gt_sb", gt)
+        word_table = sbuf("word_table", [P, T], I32)
+        nc.sync.dma_start(word_table[:], x_words[0].rearrange("p n t -> p (n t)").bitcast(I32))
+        byte_table = sbuf("byte_table", [P, T], U8)
+        nc.gpsimd.memset(byte_table[:].bitcast(I32), 0)
+        for q in range(4):
+            nc.scalar.dma_start(
+                byte_table[32 * q : 32 * q + 4, :].bitcast(I32),
+                x_scales[0, 4 * q : 4 * q + 4, :].bitcast(I32),
+            )
+        wa_raw = [load_rows(f"wa_raw{u}", wa[:, u * HALF : (u + 1) * HALF]) for u in range(2)]
+        w1_raw = load_rows("w1_raw", w1)
+        gp_sb = load_rows("gp_sb", gp)
+        n3_sb = load_list("n3_sb", n3)
+        n4_sb = load_list("n4_sb", n4)
+        n5_sb = load_list("n5_sb", n5)
+        w2_raw = load_rows("w2_raw", w2)
+        res_sb = sbuf("res_sb", [P, N // P, H], F32)
+        nc.sync.dma_start(res_sb[:], res.rearrange("(b p) j -> p b j", p=P))
+
+        picked_codes = sbuf("picked_codes", [P, S], U32)
+        picked_bytes = sbuf("picked_bytes", [P, S], U8)
+        nc.vector.tensor_copy(picked_codes[:], word_table[:].bitcast(U32).indirect(offs_sb[:]))
+        nc.vector.tensor_copy(picked_bytes[:], byte_table[:].indirect(offs_sb[:]))
+        x_codes = sbuf("x_codes", [P, S], U32)
+        x_bytes = sbuf("x_bytes", [P, S], U8)
+        for dealt, picked in ((x_codes, picked_codes), (x_bytes, picked_bytes)):
+            nc.vector.tensor_copy(
+                dealt[:].rearrange("p (t m) -> p t m", t=PACK), picked[:].rearrange("p (m t) -> p t m", t=PACK)
+            )
+
+        y_banks = [psum.tile([P, H], F32, name=f"y_bank{t}", tag=f"bank{t}") for t in range(PACK)]
+        for u in range(2):
+            wa_bf = sbuf(f"wa_bf{u}", [P, HALF, PACK], BF16)
+            nc.scalar.copy(by_lines_dst(wa_bf[:]), by_lines_src(wa_raw[u][:]))
+            wa_codes = sbuf(f"wa_codes{u}", [P, HALF], U32)
+            wa_bytes = sbuf(f"wa_bytes{u}", [P, HALF], U8)
+            quantize(nc, wa_codes[:], wa_bytes[:], wa_bf[:].rearrange("p c t -> p (c t)"))
+            for t in range(PACK):
+                rows = slice(t * P, (t + 1) * P)
+                product(nc, y_banks[t][:, u * HALF : (u + 1) * HALF], x_codes[:, rows], x_bytes[:, rows], wa_codes[:], wa_bytes[:])
+
+        w1_bf = sbuf("w1_bf", [P, PACK, P, PACK], BF16)
+
+        def group_w1(u):
+            nc.vector.tensor_copy(
+                w1_bf[:, :, u * 64 : (u + 1) * 64, :].rearrange("p i m t -> p m t i"),
+                w1_raw[:, :, u * HALF : (u + 1) * HALF].rearrange("p t (m i) -> p m t i", i=PACK),
+            )
+
+        y = [sbuf(f"y{t}", [P, H], F32) for t in range(PACK)]
+        st = [sbuf(f"st{t}", [P, H], F32) for t in range(PACK)]
+        for u in range(2):
+            plain, fused = 2 * u, 2 * u + 1
+            nc.scalar.copy(y[plain][:], y_banks[plain][:])
+            nc.scalar.copy(y[fused][:], y_banks[fused][:])
+            group_w1(u)
+            y_n1 = sbuf(f"y_n1{plain}", [P, H], F32)
+            minus_y = sbuf(f"minus_y{fused}", [P, H], F32)
+            nc.vector.tensor_scalar(minus_y[:], y[fused][:], -1.0, None, ALU.mult)
+            for start, width in chunks((HALF, HALF)):
+                cols = slice(start, start + width)
+                nc.scalar.activation(y_n1[:, cols], y[plain][:].indirect(entries(n1_sb, start, width)), ACT.Copy)
+                nc.vector.tensor_tensor(st[fused][:, cols], minus_y[:].indirect(entries(n1_sb, start, width)), y[fused][:, cols], ALU.add)
+            nc.vector.tensor_tensor(st[plain][:], y[plain][:], y_n1[:], ALU.subtract)
+
+        w1_codes = sbuf("w1_codes", [P, H], U32)
+        w1_bytes = sbuf("w1_bytes", [P, H], U8)
+        quantize(nc, w1_codes[:], w1_bytes[:], w1_bf[:].rearrange("p i m t -> p (i m t)"))
+
+        z_parts = []
+        for start, width in chunks(FIRST_HOP_CHUNKS):
+            cols = slice(start, start + width)
+            other = sbuf(f"other{start}", [P, PACK, width], F32)
+            larger = sbuf(f"larger{start}", [P, PACK, width], F32)
+            for t in (1, 0, 3, 2):
+                nc.scalar.activation(other[:, t, :], st[t][:].indirect(entries(n2_sb, start, width)), ACT.Copy)
+                nc.vector.tensor_tensor(larger[:, t, :], st[t][:, cols], other[:, t, :], ALU.max)
+            z_bf = sbuf(f"z_bf{start}", [P, width, PACK], BF16)
+            gt_all = gt_sb[:].rearrange("p t (a b) -> p a t b", a=1).to_broadcast([P, width // 4, PACK, 4])
+            nc.vector.tensor_tensor(by_lines_dst(z_bf[:]), by_lines_src(larger[:]), gt_all, ALU.mult)
+            z_codes = sbuf(f"z_codes{start}", [P, width], U32)
+            z_bytes = sbuf(f"z_bytes{start}", [P, width], U8)
+            quantize(nc, z_codes[:], z_bytes[:], z_bf[:].rearrange("p c t -> p (c t)"))
+            z_parts.append((cols, z_codes, z_bytes))
+
+        h_banks = [psum.tile([P, H], F32, name=f"h_bank{t}", tag=f"bank{PACK + t}") for t in range(PACK)]
+        for cols, z_codes, z_bytes in z_parts:
+            for t in range(PACK):
+                rows = slice(t * P, (t + 1) * P)
+                product(nc, h_banks[t][:, cols], w1_codes[:, rows], w1_bytes[:, rows], z_codes[:], z_bytes[:])
+
+        gp_flat = gp_sb[:].rearrange("p t o -> p (t o)")
+        gp_safe = sbuf("gp_safe", [P, PACK], F32)
+        nc.vector.scalar_tensor_tensor(gp_safe[:], gp_flat, 0.0, gp_flat, ALU.is_equal, ALU.add)
+        gp_inv_raw = sbuf("gp_inv_raw", [P, PACK], F32)
+        nc.vector.reciprocal(gp_inv_raw[:], gp_safe[:])
+        gp_inv = sbuf("gp_inv", [P, PACK], F32)
+        nc.vector.tensor_scalar(gp_inv[:], gp_inv_raw[:], FINITE, -FINITE, ALU.min, ALU.max)
+
+        w2_codes = sbuf("w2_codes", [P, N], U32)
+        w2_bytes = sbuf("w2_bytes", [P, N], U8)
+        for u in range(2):
+            cols = slice(u * HALF, (u + 1) * HALF)
+            w2_bf = sbuf(f"w2_bf{u}", [P, HALF, PACK], BF16, tag=("y_n12", "y2")[u])
+            nc.scalar.copy(by_lines_dst(w2_bf[:]), by_lines_src(w2_raw[:, :, cols]))
+            quantize(nc, w2_codes[:, cols], w2_bytes[:, cols], w2_bf[:].rearrange("p c t -> p (c t)"))
+
+        gh = []
+        for t in range(PACK):
+            gh.append(sbuf(f"gh{t}", [P, H], F32))
+            if t != 1:
+                nc.vector.tensor_scalar(gh[t][:], h_banks[t][:], gp_flat[:, t : t + 1], None, ALU.mult)
+            else:
+                nc.scalar.activation(gh[t][:], h_banks[t][:], ACT.Copy, scale=gp_flat[:, t : t + 1])
+
+        out_rows = out.rearrange("(b p) j -> p b j", p=P)
+        bank = 0
+        for start, width in chunks(SECOND_HOP_CHUNKS):
+            cols = slice(start, start + width)
+            pa = sbuf(f"pa{start}", [P, PACK, width], F32)
+            gate = sbuf(f"gate{start}", [P, PACK, width], F32)
+            diff = sbuf(f"diff{start}", [P, PACK, width], F32)
+            for t in range(PACK):
+                nc.scalar.activation(pa[:, t, :], gh[t][:].indirect(entries(n3_sb, start, width)), ACT.Copy)
+                if t < FUSED_SECOND:
+                    nc.vector.tensor_tensor(diff[:, t, :], gh[t][:].indirect(entries(n5_sb, start, width)), pa[:, t, :], ALU.subtract)
+                else:
+                    far = sbuf(f"far{start}_{t}", [P, width], F32)
+                    nc.scalar.activation(far[:], gh[t][:].indirect(entries(n5_sb, start, width)), ACT.Copy)
+                    nc.vector.tensor_tensor(diff[:, t, :], far[:], pa[:, t, :], ALU.subtract)
+            for t in range(PACK):
+                nc.scalar.activation(
+                    gate[:, t, :], gh[t][:].indirect(entries(n4_sb, start, width)), ACT.Sigmoid, scale=gp_inv[:, t : t + 1]
+                )
+            step = sbuf(f"step{start}", [P, PACK, width], F32)
+            nc.vector.tensor_tensor(step[:], diff[:], gate[:], ALU.mult)
+            z2_bf = sbuf(f"z2_bf{start}", [P, width, PACK], BF16)
+            nc.vector.tensor_tensor(by_lines_dst(z2_bf[:]), by_lines_src(step[:]), by_lines_src(pa[:]), ALU.add)
+            z2_codes = sbuf(f"z2_codes{start}", [P, width], U32)
+            z2_bytes = sbuf(f"z2_bytes{start}", [P, width], U8)
+            quantize(nc, z2_codes[:], z2_bytes[:], z2_bf[:].rearrange("p c t -> p (c t)"))
+            per_bank = H // width
+            for b0 in range(0, N // P, per_bank):
+                acc = psum.tile([P, per_bank, width], F32, name=f"out_bank{bank}", tag=f"bank{bank}")
+                bank = bank + 1
+                for b in range(per_bank):
+                    rows = slice((b0 + b) * P, (b0 + b + 1) * P)
+                    product(nc, acc[:, b, :], w2_codes[:, rows], w2_bytes[:, rows], z2_codes[:], z2_bytes[:])
+                total = sbuf(f"total{start}_{b0}", [P, per_bank, width], F32)
+                nc.vector.tensor_tensor(total[:], acc[:], res_sb[:, b0 : b0 + per_bank, cols], ALU.add)
+                nc.sync.dma_start(out_rows[:, b0 : b0 + per_bank, cols], total[:])

@@ -17,37 +17,33 @@ ACT = mybir.ActivationFunctionType
 
 P = 128
 PACK = 4
-PER_COL = 16
+QUADRANT = 32
+PER_COLUMN = 16
+LINE = 4
 HALF = H // 2
-FIRST_HOP_CHUNKS = (256, 128, 128)
-SECOND_HOP_CHUNKS = (128, 128, 128, 128)
-FUSED_SECOND = 3
-FINITE = 3.0e38
+CHUNK = 128
+CHUNKS = H // CHUNK
+LARGEST = 3.0e38
 
-
-def chunks(widths):
-    start = 0
-    spans = []
-    for width in widths:
-        spans.append((start, width))
-        start = start + width
-    return spans
+FUSED_ROW_TILES = 3
+EARLY_ROW_TILES = 2
+SHARED_FROM = 2
 
 
 def entries(lists, start, width):
-    return lists[:, start // PER_COL : (start + width) // PER_COL]
+    return lists[:, start // PER_COLUMN : (start + width) // PER_COLUMN]
 
 
-def by_lines_src(ap):
-    return ap.rearrange("p t (c i) -> p c t i", i=4)
+def planes_by_line(ap):
+    return ap.rearrange("p t (c i) -> p c t i", i=LINE)
 
 
-def by_lines_dst(ap):
-    return ap.rearrange("p (c i) t -> p c t i", i=4)
+def words_by_line(ap):
+    return ap.rearrange("p (c i) t -> p c t i", i=LINE)
 
 
 def quantize(nc, codes, scales, grouped):
-    nc.vector.quantize_mx(out=codes.bitcast(FP8X4), scales=scales, in_=grouped)
+    nc.vector.quantize_mx(out=codes.bitcast(FP8X4), scales=scales, in_=grouped.rearrange("p c t -> p (c t)"))
 
 
 def product(nc, acc, lhs_codes, lhs_scales, rhs_codes, rhs_scales):
@@ -66,15 +62,17 @@ def tile_picked_tok2hopmxlerp_none_p_kernel(
     tc, x_words, x_scales, wa, gt, w1, gp, res, w2, offs, n1, n2, n3, n4, n5, out
 ):
     nc = tc.nc
+    halves = [slice(u * HALF, (u + 1) * HALF) for u in range(2)]
+    blocks = [slice(b * P, (b + 1) * P) for b in range(PACK)]
     with ExitStack() as ctx:
         keep = ctx.enter_context(tc.tile_pool(name="keep", bufs=1))
         psum = ctx.enter_context(tc.psum_pool(name="psum", bufs=1))
 
-        def sbuf(name, shape, dtype, tag=None):
-            return keep.tile(shape, dtype, name=name, tag=tag or name, align_bytes=64)
+        def sbuf(name, shape, dtype, reuses=None):
+            return keep.tile(shape, dtype, name=name, tag=reuses or name, align_bytes=64)
 
         def load_list(name, lists):
-            tile = keep.tile([P, S // PER_COL], U16, name=name)
+            tile = keep.tile([P, S // PER_COLUMN], U16, name=name)
             nc.sync.dma_start(tile[:], lists)
             return tile
 
@@ -83,22 +81,26 @@ def tile_picked_tok2hopmxlerp_none_p_kernel(
             nc.sync.dma_start(tile[:], rows.rearrange("(p t) c -> p t c", t=PACK))
             return tile
 
+        def fetch(dst, window, lists, start, width):
+            nc.scalar.activation(dst, window[:].indirect(entries(lists, start, width)), ACT.Copy)
+
         offs_sb = load_list("offs_sb", offs)
         n1_sb = load_list("n1_sb", n1)
+        wa_raw = [load_rows(f"wa_raw{u}", wa[:, cols]) for u, cols in enumerate(halves)]
         n2_sb = load_list("n2_sb", n2)
-        gt_sb = load_rows("gt_sb", gt)
-        word_table = sbuf("word_table", [P, T], I32)
-        nc.sync.dma_start(word_table[:], x_words[0].rearrange("p n t -> p (n t)").bitcast(I32))
         byte_table = sbuf("byte_table", [P, T], U8)
         nc.gpsimd.memset(byte_table[:].bitcast(I32), 0)
-        for q in range(4):
+        for q in range(P // QUADRANT):
             nc.scalar.dma_start(
-                byte_table[32 * q : 32 * q + 4, :].bitcast(I32),
+                byte_table[QUADRANT * q : QUADRANT * q + 4, :].bitcast(I32),
                 x_scales[0, 4 * q : 4 * q + 4, :].bitcast(I32),
             )
-        wa_raw = [load_rows(f"wa_raw{u}", wa[:, u * HALF : (u + 1) * HALF]) for u in range(2)]
-        w1_raw = load_rows("w1_raw", w1)
+        word_table = sbuf("word_table", [P, T], I32)
+        nc.sync.dma_start(word_table[:], x_words[0].rearrange("p n t -> p (n t)").bitcast(I32))
         gp_sb = load_rows("gp_sb", gp)
+        w1_pieces = [slice(0, H // 4), slice(H // 4, HALF), slice(HALF, H)]
+        w1_raw = [load_rows(f"w1_raw{u}", w1[:, cols]) for u, cols in enumerate(w1_pieces)]
+        gt_sb = load_rows("gt_sb", gt)
         n3_sb = load_list("n3_sb", n3)
         n4_sb = load_list("n4_sb", n4)
         n5_sb = load_list("n5_sb", n5)
@@ -106,135 +108,169 @@ def tile_picked_tok2hopmxlerp_none_p_kernel(
         res_sb = sbuf("res_sb", [P, N // P, H], F32)
         nc.sync.dma_start(res_sb[:], res.rearrange("(b p) j -> p b j", p=P))
 
-        picked_codes = sbuf("picked_codes", [P, S], U32)
-        picked_bytes = sbuf("picked_bytes", [P, S], U8)
-        nc.vector.tensor_copy(picked_codes[:], word_table[:].bitcast(U32).indirect(offs_sb[:]))
-        nc.vector.tensor_copy(picked_bytes[:], byte_table[:].indirect(offs_sb[:]))
-        x_codes = sbuf("x_codes", [P, S], U32)
-        x_bytes = sbuf("x_bytes", [P, S], U8)
-        for dealt, picked in ((x_codes, picked_codes), (x_bytes, picked_bytes)):
-            nc.vector.tensor_copy(
-                dealt[:].rearrange("p (t m) -> p t m", t=PACK), picked[:].rearrange("p (m t) -> p t m", t=PACK)
-            )
+        def dealt(ap):
+            return ap.rearrange("p (t m) -> p t m", t=PACK)
 
-        y_banks = [psum.tile([P, H], F32, name=f"y_bank{t}", tag=f"bank{t}") for t in range(PACK)]
-        for u in range(2):
+        def in_list_order(ap):
+            return ap.rearrange("p (m t) -> p t m", t=PACK)
+
+        picked_bytes = sbuf("picked_bytes", [P, S], U8)
+        nc.vector.tensor_copy(picked_bytes[:], byte_table[:].indirect(offs_sb[:]))
+        x_bytes = sbuf("x_bytes", [P, S], U8)
+        nc.vector.tensor_copy(dealt(x_bytes[:]), in_list_order(picked_bytes[:]))
+
+        wa_codes = sbuf("wa_codes", [P, H], U32)
+        wa_bytes = sbuf("wa_bytes", [P, H], U8)
+        for u, cols in enumerate(halves):
             wa_bf = sbuf(f"wa_bf{u}", [P, HALF, PACK], BF16)
-            nc.scalar.copy(by_lines_dst(wa_bf[:]), by_lines_src(wa_raw[u][:]))
-            wa_codes = sbuf(f"wa_codes{u}", [P, HALF], U32)
-            wa_bytes = sbuf(f"wa_bytes{u}", [P, HALF], U8)
-            quantize(nc, wa_codes[:], wa_bytes[:], wa_bf[:].rearrange("p c t -> p (c t)"))
-            for t in range(PACK):
-                rows = slice(t * P, (t + 1) * P)
-                product(nc, y_banks[t][:, u * HALF : (u + 1) * HALF], x_codes[:, rows], x_bytes[:, rows], wa_codes[:], wa_bytes[:])
+            nc.scalar.copy(words_by_line(wa_bf[:]), planes_by_line(wa_raw[u][:]))
+            quantize(nc, wa_codes[:, cols], wa_bytes[:, cols], wa_bf[:])
+
+        picked_codes = sbuf("picked_codes", [P, S], U32)
+        nc.vector.tensor_copy(picked_codes[:], word_table[:].bitcast(U32).indirect(offs_sb[:]))
+        x_codes = sbuf("x_codes", [P, S], U32)
+        for tiles in (slice(0, 1), slice(1, PACK)):
+            nc.vector.tensor_copy(dealt(x_codes[:])[:, tiles, :], in_list_order(picked_codes[:])[:, tiles, :])
+        y_banks = [psum.tile([P, H], F32, name=f"y_bank{t}", tag=f"bank{t}") for t in range(PACK)]
+        for t in range(PACK):
+            product(nc, y_banks[t][:], x_codes[:, blocks[t]], x_bytes[:, blocks[t]], wa_codes[:], wa_bytes[:])
+
+        gp_cols = gp_sb[:].rearrange("p t o -> p (t o)")
+        gp_nonzero = sbuf("gp_nonzero", [P, PACK], F32)
+        nc.vector.scalar_tensor_tensor(gp_nonzero[:], gp_cols, 0.0, gp_cols, ALU.is_equal, ALU.add)
+        gp_reciprocal = sbuf("gp_reciprocal", [P, PACK], F32)
+        nc.vector.reciprocal(gp_reciprocal[:], gp_nonzero[:])
+        undo_gp = sbuf("undo_gp", [P, PACK], F32)
+        nc.vector.tensor_scalar(undo_gp[:], gp_reciprocal[:], LARGEST, -LARGEST, ALU.min, ALU.max)
 
         w1_bf = sbuf("w1_bf", [P, PACK, P, PACK], BF16)
-
-        def group_w1(u):
-            nc.vector.tensor_copy(
-                w1_bf[:, :, u * 64 : (u + 1) * 64, :].rearrange("p i m t -> p m t i"),
-                w1_raw[:, :, u * HALF : (u + 1) * HALF].rearrange("p t (m i) -> p m t i", i=PACK),
+        for raw, cols, copy in zip(w1_raw, w1_pieces, (nc.scalar.copy, nc.scalar.copy, nc.vector.tensor_copy)):
+            copy(
+                w1_bf[:, :, cols.start // PACK : cols.stop // PACK, :].rearrange("p i m t -> p m t i"),
+                raw[:].rearrange("p t (m i) -> p m t i", i=PACK),
             )
-
-        y = [sbuf(f"y{t}", [P, H], F32) for t in range(PACK)]
-        st = [sbuf(f"st{t}", [P, H], F32) for t in range(PACK)]
-        for u in range(2):
-            plain, fused = 2 * u, 2 * u + 1
-            nc.scalar.copy(y[plain][:], y_banks[plain][:])
-            nc.scalar.copy(y[fused][:], y_banks[fused][:])
-            group_w1(u)
-            y_n1 = sbuf(f"y_n1{plain}", [P, H], F32)
-            minus_y = sbuf(f"minus_y{fused}", [P, H], F32)
-            nc.vector.tensor_scalar(minus_y[:], y[fused][:], -1.0, None, ALU.mult)
-            for start, width in chunks((HALF, HALF)):
-                cols = slice(start, start + width)
-                nc.scalar.activation(y_n1[:, cols], y[plain][:].indirect(entries(n1_sb, start, width)), ACT.Copy)
-                nc.vector.tensor_tensor(st[fused][:, cols], minus_y[:].indirect(entries(n1_sb, start, width)), y[fused][:, cols], ALU.add)
-            nc.vector.tensor_tensor(st[plain][:], y[plain][:], y_n1[:], ALU.subtract)
-
         w1_codes = sbuf("w1_codes", [P, H], U32)
         w1_bytes = sbuf("w1_bytes", [P, H], U8)
-        quantize(nc, w1_codes[:], w1_bytes[:], w1_bf[:].rearrange("p i m t -> p (i m t)"))
+        quantize(nc, w1_codes[:], w1_bytes[:], w1_bf[:].rearrange("p i m t -> p (i m) t"))
 
+        st = [sbuf(f"st{t}", [P, H], F32) for t in range(PACK)]
+        y_fused = sbuf("y_fused", [P, FUSED_ROW_TILES, H], F32, reuses="w1_raw0")
+        for t in range(PACK):
+            if t < FUSED_ROW_TILES:
+                y = y_fused[:, t, :]
+                nc.scalar.copy(y, y_banks[t][:])
+                minus_y = sbuf(f"minus_y{t}", [P, H], F32)
+                nc.vector.tensor_scalar(minus_y[:], y, -1.0, None, ALU.mult)
+                for cols in halves:
+                    looked_up = minus_y[:].indirect(entries(n1_sb, cols.start, HALF))
+                    nc.vector.tensor_tensor(st[t][:, cols], looked_up, y[:, cols], ALU.add)
+            else:
+                y = sbuf(f"y{t}", [P, H], F32, reuses="w1_raw1")
+                nc.scalar.copy(y[:], y_banks[t][:])
+                y_n1 = sbuf(f"y_n1_{t}", [P, H], F32)
+                for cols in halves:
+                    fetch(y_n1[:, cols], y, n1_sb, cols.start, HALF)
+                nc.vector.tensor_tensor(st[t][:], y[:], y_n1[:], ALU.subtract)
+        last_y, last_y_n1 = "w1_raw1", f"y_n1_{PACK - 1}"
+
+        larger = sbuf("larger", [P, CHUNKS, PACK, CHUNK], F32)
+        late_tiles = PACK - EARLY_ROW_TILES
+        st_n2_first = sbuf("st_n2_first", [P, late_tiles, CHUNK], F32)
+        st_n2_rest = sbuf("st_n2_rest", [P, late_tiles, H - CHUNK], F32, reuses=last_y)
+        for t in range(EARLY_ROW_TILES):
+            st_n2 = sbuf(f"st_n2_{t}", [P, H], F32)
+            for cols in halves:
+                fetch(st_n2[:, cols], st[t], n2_sb, cols.start, HALF)
+            nc.vector.tensor_tensor(
+                larger[:, :, t, :],
+                st[t][:].rearrange("p (c j) -> p c j", j=CHUNK),
+                st_n2[:].rearrange("p (c j) -> p c j", j=CHUNK),
+                ALU.max,
+            )
+        gt_by_line = gt_sb[:].rearrange("p t (c i) -> p c t i", c=1).to_broadcast([P, CHUNK // LINE, PACK, LINE])
         z_parts = []
-        for start, width in chunks(FIRST_HOP_CHUNKS):
-            cols = slice(start, start + width)
-            other = sbuf(f"other{start}", [P, PACK, width], F32)
-            larger = sbuf(f"larger{start}", [P, PACK, width], F32)
-            for t in (1, 0, 3, 2):
-                nc.scalar.activation(other[:, t, :], st[t][:].indirect(entries(n2_sb, start, width)), ACT.Copy)
-                nc.vector.tensor_tensor(larger[:, t, :], st[t][:, cols], other[:, t, :], ALU.max)
-            z_bf = sbuf(f"z_bf{start}", [P, width, PACK], BF16)
-            gt_all = gt_sb[:].rearrange("p t (a b) -> p a t b", a=1).to_broadcast([P, width // 4, PACK, 4])
-            nc.vector.tensor_tensor(by_lines_dst(z_bf[:]), by_lines_src(larger[:]), gt_all, ALU.mult)
-            z_codes = sbuf(f"z_codes{start}", [P, width], U32)
-            z_bytes = sbuf(f"z_bytes{start}", [P, width], U8)
-            quantize(nc, z_codes[:], z_bytes[:], z_bf[:].rearrange("p c t -> p (c t)"))
-            z_parts.append((cols, z_codes, z_bytes))
+        for c in range(CHUNKS):
+            start = c * CHUNK
+            for late in range(late_tiles):
+                t = EARLY_ROW_TILES + late
+                fetched = st_n2_first[:, late, :] if c == 0 else st_n2_rest[:, late, start - CHUNK : start]
+                fetch(fetched, st[t], n2_sb, start, CHUNK)
+                nc.vector.tensor_tensor(larger[:, c, t, :], st[t][:, start : start + CHUNK], fetched, ALU.max)
+            z_bf = sbuf(f"z_bf{c}", [P, CHUNK, PACK], BF16)
+            nc.vector.tensor_tensor(words_by_line(z_bf[:]), planes_by_line(larger[:, c, :, :]), gt_by_line, ALU.mult)
+            z_codes = sbuf(f"z_codes{c}", [P, CHUNK], U32)
+            z_bytes = sbuf(f"z_bytes{c}", [P, CHUNK], U8)
+            quantize(nc, z_codes[:], z_bytes[:], z_bf[:])
+            z_parts.append((z_codes, z_bytes))
 
         h_banks = [psum.tile([P, H], F32, name=f"h_bank{t}", tag=f"bank{PACK + t}") for t in range(PACK)]
-        for cols, z_codes, z_bytes in z_parts:
+        for c, (z_codes, z_bytes) in enumerate(z_parts):
             for t in range(PACK):
-                rows = slice(t * P, (t + 1) * P)
-                product(nc, h_banks[t][:, cols], w1_codes[:, rows], w1_bytes[:, rows], z_codes[:], z_bytes[:])
-
-        gp_flat = gp_sb[:].rearrange("p t o -> p (t o)")
-        gp_safe = sbuf("gp_safe", [P, PACK], F32)
-        nc.vector.scalar_tensor_tensor(gp_safe[:], gp_flat, 0.0, gp_flat, ALU.is_equal, ALU.add)
-        gp_inv_raw = sbuf("gp_inv_raw", [P, PACK], F32)
-        nc.vector.reciprocal(gp_inv_raw[:], gp_safe[:])
-        gp_inv = sbuf("gp_inv", [P, PACK], F32)
-        nc.vector.tensor_scalar(gp_inv[:], gp_inv_raw[:], FINITE, -FINITE, ALU.min, ALU.max)
+                acc = h_banks[t][:, c * CHUNK : (c + 1) * CHUNK]
+                product(nc, acc, w1_codes[:, blocks[t]], w1_bytes[:, blocks[t]], z_codes[:], z_bytes[:])
 
         w2_codes = sbuf("w2_codes", [P, N], U32)
         w2_bytes = sbuf("w2_bytes", [P, N], U8)
-        for u in range(2):
-            cols = slice(u * HALF, (u + 1) * HALF)
-            w2_bf = sbuf(f"w2_bf{u}", [P, HALF, PACK], BF16, tag=("y_n12", "y2")[u])
-            nc.scalar.copy(by_lines_dst(w2_bf[:]), by_lines_src(w2_raw[:, :, cols]))
-            quantize(nc, w2_codes[:, cols], w2_bytes[:, cols], w2_bf[:].rearrange("p c t -> p (c t)"))
+        w2_bf = sbuf("w2_bf", [P, N, PACK], BF16, reuses=last_y_n1)
+        for cols in halves:
+            nc.scalar.copy(words_by_line(w2_bf[:, cols, :]), planes_by_line(w2_raw[:, :, cols]))
+            quantize(nc, w2_codes[:, cols], w2_bytes[:, cols], w2_bf[:, cols, :])
 
-        gh = []
+        gh = [sbuf(f"gh{t}", [P, H], F32) for t in range(PACK)]
         for t in range(PACK):
-            gh.append(sbuf(f"gh{t}", [P, H], F32))
-            if t != 1:
-                nc.vector.tensor_scalar(gh[t][:], h_banks[t][:], gp_flat[:, t : t + 1], None, ALU.mult)
-            else:
-                nc.scalar.activation(gh[t][:], h_banks[t][:], ACT.Copy, scale=gp_flat[:, t : t + 1])
+            nc.vector.tensor_scalar(gh[t][:], h_banks[t][:], gp_cols[:, t : t + 1], None, ALU.mult)
 
         out_rows = out.rearrange("(b p) j -> p b j", p=P)
-        bank = 0
-        for start, width in chunks(SECOND_HOP_CHUNKS):
-            cols = slice(start, start + width)
-            pa = sbuf(f"pa{start}", [P, PACK, width], F32)
-            gate = sbuf(f"gate{start}", [P, PACK, width], F32)
-            diff = sbuf(f"diff{start}", [P, PACK, width], F32)
+
+        def finish(c, z2_codes, z2_bytes, row_blocks, bank, reuses=None):
+            cols = slice(c * CHUNK, (c + 1) * CHUNK)
+            count = row_blocks.stop - row_blocks.start
+            acc = psum.tile([P, count, CHUNK], F32, name=f"out_bank{bank}", tag=f"bank{bank}")
+            for b in range(count):
+                rows = blocks[row_blocks.start + b]
+                product(nc, acc[:, b, :], w2_codes[:, rows], w2_bytes[:, rows], z2_codes[:], z2_bytes[:])
+            total = sbuf(f"total{bank}", [P, count, CHUNK], F32, reuses=reuses)
+            nc.vector.tensor_tensor(total[:], acc[:], res_sb[:, row_blocks, cols], ALU.add)
+            nc.sync.dma_start(out_rows[:, row_blocks, cols], total[:])
+
+        z2_parts = []
+        for c in range(CHUNKS):
+            start = c * CHUNK
+            pa_gate = sbuf(f"pa_gate{c}", [P, 2, PACK, CHUNK], F32)
+            pa, gate = pa_gate[:, 0, :, :], pa_gate[:, 1, :, :]
+            diff = sbuf(f"diff{c}", [P, PACK, CHUNK], F32)
+
+            def fetch_gate(t):
+                looked_up = gh[t][:].indirect(entries(n4_sb, start, CHUNK))
+                nc.scalar.activation(gate[:, t, :], looked_up, ACT.Sigmoid, scale=undo_gp[:, t : t + 1])
+
+            gates_ahead = 1 if c == 0 else 0
+            for t in range(gates_ahead):
+                fetch_gate(t)
             for t in range(PACK):
-                nc.scalar.activation(pa[:, t, :], gh[t][:].indirect(entries(n3_sb, start, width)), ACT.Copy)
-                if t < FUSED_SECOND:
-                    nc.vector.tensor_tensor(diff[:, t, :], gh[t][:].indirect(entries(n5_sb, start, width)), pa[:, t, :], ALU.subtract)
+                fetch(pa[:, t, :], gh[t], n3_sb, start, CHUNK)
+                if c >= SHARED_FROM and t >= SHARED_FROM:
+                    gh_n5 = sbuf(f"gh_n5_{c}_{t}", [P, CHUNK], F32)
+                    fetch(gh_n5[:], gh[t], n5_sb, start, CHUNK)
+                    far = gh_n5[:]
                 else:
-                    far = sbuf(f"far{start}_{t}", [P, width], F32)
-                    nc.scalar.activation(far[:], gh[t][:].indirect(entries(n5_sb, start, width)), ACT.Copy)
-                    nc.vector.tensor_tensor(diff[:, t, :], far[:], pa[:, t, :], ALU.subtract)
-            for t in range(PACK):
-                nc.scalar.activation(
-                    gate[:, t, :], gh[t][:].indirect(entries(n4_sb, start, width)), ACT.Sigmoid, scale=gp_inv[:, t : t + 1]
-                )
-            step = sbuf(f"step{start}", [P, PACK, width], F32)
-            nc.vector.tensor_tensor(step[:], diff[:], gate[:], ALU.mult)
-            z2_bf = sbuf(f"z2_bf{start}", [P, width, PACK], BF16)
-            nc.vector.tensor_tensor(by_lines_dst(z2_bf[:]), by_lines_src(step[:]), by_lines_src(pa[:]), ALU.add)
-            z2_codes = sbuf(f"z2_codes{start}", [P, width], U32)
-            z2_bytes = sbuf(f"z2_bytes{start}", [P, width], U8)
-            quantize(nc, z2_codes[:], z2_bytes[:], z2_bf[:].rearrange("p c t -> p (c t)"))
-            per_bank = H // width
-            for b0 in range(0, N // P, per_bank):
-                acc = psum.tile([P, per_bank, width], F32, name=f"out_bank{bank}", tag=f"bank{bank}")
-                bank = bank + 1
-                for b in range(per_bank):
-                    rows = slice((b0 + b) * P, (b0 + b + 1) * P)
-                    product(nc, acc[:, b, :], w2_codes[:, rows], w2_bytes[:, rows], z2_codes[:], z2_bytes[:])
-                total = sbuf(f"total{start}_{b0}", [P, per_bank, width], F32)
-                nc.vector.tensor_tensor(total[:], acc[:], res_sb[:, b0 : b0 + per_bank, cols], ALU.add)
-                nc.sync.dma_start(out_rows[:, b0 : b0 + per_bank, cols], total[:])
+                    far = gh[t][:].indirect(entries(n5_sb, start, CHUNK))
+                nc.vector.tensor_tensor(diff[:, t, :], far, pa[:, t, :], ALU.subtract)
+            for t in range(gates_ahead, PACK):
+                fetch_gate(t)
+            step = sbuf(f"step{c}", [P, PACK, CHUNK], F32)
+            for pair in (slice(0, 2), slice(2, 4)):
+                nc.vector.tensor_tensor(step[:, pair, :], diff[:, pair, :], gate[:, pair, :], ALU.mult)
+            z2_bf = sbuf(f"z2_bf{c}", [P, CHUNK, PACK], BF16)
+            nc.vector.tensor_tensor(words_by_line(z2_bf[:]), planes_by_line(step[:]), planes_by_line(pa), ALU.add)
+            z2_codes = sbuf(f"z2_codes{c}", [P, CHUNK], U32)
+            z2_bytes = sbuf(f"z2_bytes{c}", [P, CHUNK], U8)
+            quantize(nc, z2_codes[:], z2_bytes[:], z2_bf[:])
+            z2_parts.append((z2_codes, z2_bytes))
+            if c < CHUNKS - 2:
+                finish(c, z2_codes, z2_bytes, slice(0, PACK), bank=c)
+
+        last = CHUNKS - 1
+        finish(last - 1, *z2_parts[last - 1], slice(0, PACK), bank=last - 1, reuses=f"z2_bf{last}")
+        finish(last, *z2_parts[last], slice(0, 2), bank=last)
+        finish(last, *z2_parts[last], slice(2, 4), bank=last + 1)

@@ -233,11 +233,13 @@ def tile_picked_tok2hopmxlerp_none_p_kernel(
             nc.vector.tensor_tensor(total[:], acc[:], res_sb[:, row_blocks, cols], ALU.add)
             nc.sync.dma_start(out_rows[:, row_blocks, cols], total[:])
 
+        fetched_first = sbuf("fetched_first", [P, 2, PACK, CHUNK], F32)
+        fetched_rest = sbuf("fetched_rest", [P, CHUNKS - 1, 3, PACK, CHUNK], F32, reuses="gp_sb")
         z2_parts = []
         for c in range(CHUNKS):
             start = c * CHUNK
-            pa_gate = sbuf(f"pa_gate{c}", [P, 2, PACK, CHUNK], F32)
-            pa, gate = pa_gate[:, 0, :, :], pa_gate[:, 1, :, :]
+            fetched = fetched_first[:] if c == 0 else fetched_rest[:, c - 1, :, :, :]
+            pa, gate = fetched[:, 0, :, :], fetched[:, 1, :, :]
             diff = sbuf(f"diff{c}", [P, PACK, CHUNK], F32)
 
             def fetch_gate(t):
@@ -249,10 +251,9 @@ def tile_picked_tok2hopmxlerp_none_p_kernel(
                 fetch_gate(t)
             for t in range(PACK):
                 fetch(pa[:, t, :], gh[t], n3_sb, start, CHUNK)
-                if c >= SHARED_FROM and t >= SHARED_FROM:
-                    gh_n5 = sbuf(f"gh_n5_{c}_{t}", [P, CHUNK], F32)
-                    fetch(gh_n5[:], gh[t], n5_sb, start, CHUNK)
-                    far = gh_n5[:]
+                if c >= SHARED_FROM and t == PACK - 1:
+                    far = fetched[:, 2, t, :]
+                    fetch(far, gh[t], n5_sb, start, CHUNK)
                 else:
                     far = gh[t][:].indirect(entries(n5_sb, start, CHUNK))
                 nc.vector.tensor_tensor(diff[:, t, :], far, pa[:, t, :], ALU.subtract)

@@ -19,7 +19,7 @@ P = 128
 PACK = 4
 QUADRANT = 32
 PER_COLUMN = 16
-LINE = 4
+LINE = 2
 HALF = H // 2
 CHUNK = 128
 CHUNKS = H // CHUNK
@@ -146,8 +146,8 @@ def tile_picked_tok2hopmxlerp_none_p_kernel(
         w1_bf = sbuf("w1_bf", [P, PACK, P, PACK], BF16)
         for raw, cols, copy in zip(w1_raw, w1_pieces, (nc.scalar.copy, nc.scalar.copy, nc.vector.tensor_copy)):
             copy(
-                w1_bf[:, :, cols.start // PACK : cols.stop // PACK, :].rearrange("p i m t -> p m t i"),
-                raw[:].rearrange("p t (m i) -> p m t i", i=PACK),
+                w1_bf[:, :, cols.start // PACK : cols.stop // PACK, :].rearrange("p i m t -> p m i t"),
+                raw[:].rearrange("p t (m i) -> p m i t", i=PACK),
             )
         w1_codes = sbuf("w1_codes", [P, H], U32)
         w1_bytes = sbuf("w1_bytes", [P, H], U8)

from contextlib import ExitStack

import concourse.mybir as mybir

K, T, S, H, N = 512, 2048, 512, 512, 512
FLOPS = 2 * (K * S * H + S * H * H + H * N * H)

F32 = mybir.dt.float32
BF16 = mybir.dt.bfloat16
I32 = mybir.dt.int32
U32 = mybir.dt.uint32
U16 = mybir.dt.uint16
U8 = mybir.dt.uint8
FP8X4 = mybir.dt.float8_e4m3fn_x4
ALU = mybir.AluOpType
ACT = mybir.ActivationFunctionType

P = 128
PACK = 4
QUADRANT = 32
PER_COLUMN = 16
LINE = 2
HALF = H // 2
CHUNK = 128
CHUNKS = H // CHUNK
LARGEST = 3.0e38

FUSED_ROW_TILES = 3
EARLY_ROW_TILES = 2
SHARED_FROM = 2


def entries(lists, start, width):
    return lists[:, start // PER_COLUMN : (start + width) // PER_COLUMN]


def planes_by_line(ap):
    return ap.rearrange("p t (c i) -> p c t i", i=LINE)


def words_by_line(ap):
    return ap.rearrange("p (c i) t -> p c t i", i=LINE)


def quantize(nc, codes, scales, grouped):
    nc.vector.quantize_mx(out=codes.bitcast(FP8X4), scales=scales, in_=grouped.rearrange("p c t -> p (c t)"))


def product(nc, acc, lhs_codes, lhs_scales, rhs_codes, rhs_scales):
    nc.tensor.matmul_mx(
        out=acc,
        lhsT=lhs_codes.bitcast(FP8X4),
        lhsT_scale=lhs_scales,
        rhs=rhs_codes.bitcast(FP8X4),
        rhs_scale=rhs_scales,
        start=True,
        stop=True,
    )


def tile_picked_tok2hopmxlerp_none_p_kernel(
    tc, x_words, x_scales, wa, gt, w1, gp, res, w2, offs, n1, n2, n3, n4, n5, out
):
    nc = tc.nc
    halves = [slice(u * HALF, (u + 1) * HALF) for u in range(2)]
    blocks = [slice(b * P, (b + 1) * P) for b in range(PACK)]
    with ExitStack() as ctx:
        keep = ctx.enter_context(tc.tile_pool(name="keep", bufs=1))
        psum = ctx.enter_context(tc.psum_pool(name="psum", bufs=1))

        def sbuf(name, shape, dtype, reuses=None):
            return keep.tile(shape, dtype, name=name, tag=reuses or name, align_bytes=64)

        def load_list(name, lists):
            tile = keep.tile([P, S // PER_COLUMN], U16, name=name)
            nc.sync.dma_start(tile[:], lists)
            return tile

        def load_rows(name, rows):
            tile = sbuf(name, [P, PACK, rows.shape[1]], F32)
            nc.sync.dma_start(tile[:], rows.rearrange("(p t) c -> p t c", t=PACK))
            return tile

        def fetch(dst, window, lists, start, width):
            nc.scalar.activation(dst, window[:].indirect(entries(lists, start, width)), ACT.Copy)

        offs_sb = load_list("offs_sb", offs)
        n1_sb = load_list("n1_sb", n1)
        wa_raw = [load_rows(f"wa_raw{u}", wa[:, cols]) for u, cols in enumerate(halves)]
        n2_sb = load_list("n2_sb", n2)
        byte_table = sbuf("byte_table", [P, T], U8)
        nc.gpsimd.memset(byte_table[:].bitcast(I32), 0)
        for q in range(P // QUADRANT):
            nc.scalar.dma_start(
                byte_table[QUADRANT * q : QUADRANT * q + 4, :].bitcast(I32),
                x_scales[0, 4 * q : 4 * q + 4, :].bitcast(I32),
            )
        word_table = sbuf("word_table", [P, T], I32)
        nc.sync.dma_start(word_table[:], x_words[0].rearrange("p n t -> p (n t)").bitcast(I32))
        gp_sb = load_rows("gp_sb", gp)
        w1_pieces = [slice(0, H // 4), slice(H // 4, HALF), slice(HALF, H)]
        w1_raw = [load_rows(f"w1_raw{u}", w1[:, cols]) for u, cols in enumerate(w1_pieces)]
        gt_sb = load_rows("gt_sb", gt)
        n3_sb = load_list("n3_sb", n3)
        n4_sb = load_list("n4_sb", n4)
        n5_sb = load_list("n5_sb", n5)
        w2_raw = load_rows("w2_raw", w2)
        res_sb = sbuf("res_sb", [P, N // P, H], F32)
        nc.sync.dma_start(res_sb[:], res.rearrange("(b p) j -> p b j", p=P))

        def dealt(ap):
            return ap.rearrange("p (t m) -> p t m", t=PACK)

        def in_list_order(ap):
            return ap.rearrange("p (m t) -> p t m", t=PACK)

        picked_bytes = sbuf("picked_bytes", [P, S], U8)
        nc.vector.tensor_copy(picked_bytes[:], byte_table[:].indirect(offs_sb[:]))
        x_bytes = sbuf("x_bytes", [P, S], U8)
        nc.vector.tensor_copy(dealt(x_bytes[:]), in_list_order(picked_bytes[:]))

        wa_codes = sbuf("wa_codes", [P, H], U32)
        wa_bytes = sbuf("wa_bytes", [P, H], U8)
        for u, cols in enumerate(halves):
            wa_bf = sbuf(f"wa_bf{u}", [P, HALF, PACK], BF16)
            nc.scalar.copy(words_by_line(wa_bf[:]), planes_by_line(wa_raw[u][:]))
            quantize(nc, wa_codes[:, cols], wa_bytes[:, cols], wa_bf[:])

        picked_codes = sbuf("picked_codes", [P, S], U32)
        nc.vector.tensor_copy(picked_codes[:], word_table[:].bitcast(U32).indirect(offs_sb[:]))
        x_codes = sbuf("x_codes", [P, S], U32)
        for tiles in (slice(0, 1), slice(1, PACK)):
            nc.vector.tensor_copy(dealt(x_codes[:])[:, tiles, :], in_list_order(picked_codes[:])[:, tiles, :])
        y_banks = [psum.tile([P, H], F32, name=f"y_bank{t}", tag=f"bank{t}") for t in range(PACK)]
        for t in range(PACK):
            product(nc, y_banks[t][:], x_codes[:, blocks[t]], x_bytes[:, blocks[t]], wa_codes[:], wa_bytes[:])

        gp_cols = gp_sb[:].rearrange("p t o -> p (t o)")
        gp_nonzero = sbuf("gp_nonzero", [P, PACK], F32)
        nc.vector.scalar_tensor_tensor(gp_nonzero[:], gp_cols, 0.0, gp_cols, ALU.is_equal, ALU.add)
        gp_reciprocal = sbuf("gp_reciprocal", [P, PACK], F32)
        nc.vector.reciprocal(gp_reciprocal[:], gp_nonzero[:])
        undo_gp = sbuf("undo_gp", [P, PACK], F32)
        nc.vector.tensor_scalar(undo_gp[:], gp_reciprocal[:], LARGEST, -LARGEST, ALU.min, ALU.max)

        w1_bf = sbuf("w1_bf", [P, PACK, P, PACK], BF16)
        for raw, cols, copy in zip(w1_raw, w1_pieces, (nc.scalar.copy, nc.scalar.copy, nc.vector.tensor_copy)):
            copy(
                w1_bf[:, :, cols.start // PACK : cols.stop // PACK, :].rearrange("p i m t -> p m i t"),
                raw[:].rearrange("p t (m i) -> p m i t", i=PACK),
            )
        w1_codes = sbuf("w1_codes", [P, H], U32)
        w1_bytes = sbuf("w1_bytes", [P, H], U8)
        quantize(nc, w1_codes[:], w1_bytes[:], w1_bf[:].rearrange("p i m t -> p (i m) t"))

        st = [sbuf(f"st{t}", [P, H], F32) for t in range(PACK)]
        y_fused = sbuf("y_fused", [P, FUSED_ROW_TILES, H], F32, reuses="w1_raw0")
        for t in range(PACK):
            if t < FUSED_ROW_TILES:
                y = y_fused[:, t, :]
                nc.scalar.copy(y, y_banks[t][:])
                minus_y = sbuf(f"minus_y{t}", [P, H], F32)
                nc.vector.tensor_scalar(minus_y[:], y, -1.0, None, ALU.mult)
                for cols in halves:
                    looked_up = minus_y[:].indirect(entries(n1_sb, cols.start, HALF))
                    nc.vector.tensor_tensor(st[t][:, cols], looked_up, y[:, cols], ALU.add)
            else:
                y = sbuf(f"y{t}", [P, H], F32, reuses="w1_raw1")
                nc.scalar.copy(y[:], y_banks[t][:])
                y_n1 = sbuf(f"y_n1_{t}", [P, H], F32)
                for cols in halves:
                    fetch(y_n1[:, cols], y, n1_sb, cols.start, HALF)
                nc.vector.tensor_tensor(st[t][:], y[:], y_n1[:], ALU.subtract)
        last_y, last_y_n1 = "w1_raw1", f"y_n1_{PACK - 1}"

        larger = sbuf("larger", [P, CHUNKS, PACK, CHUNK], F32)
        late_tiles = PACK - EARLY_ROW_TILES
        st_n2_first = sbuf("st_n2_first", [P, late_tiles, CHUNK], F32)
        st_n2_rest = sbuf("st_n2_rest", [P, late_tiles, H - CHUNK], F32, reuses=last_y)
        for t in range(EARLY_ROW_TILES):
            st_n2 = sbuf(f"st_n2_{t}", [P, H], F32)
            for cols in halves:
                fetch(st_n2[:, cols], st[t], n2_sb, cols.start, HALF)
            nc.vector.tensor_tensor(
                larger[:, :, t, :],
                st[t][:].rearrange("p (c j) -> p c j", j=CHUNK),
                st_n2[:].rearrange("p (c j) -> p c j", j=CHUNK),
                ALU.max,
            )
        gt_by_line = gt_sb[:].rearrange("p t (c i) -> p c t i", c=1).to_broadcast([P, CHUNK // LINE, PACK, LINE])
        z_parts = []
        for c in range(CHUNKS):
            start = c * CHUNK
            for late in range(late_tiles):
                t = EARLY_ROW_TILES + late
                fetched = st_n2_first[:, late, :] if c == 0 else st_n2_rest[:, late, start - CHUNK : start]
                fetch(fetched, st[t], n2_sb, start, CHUNK)
                nc.vector.tensor_tensor(larger[:, c, t, :], st[t][:, start : start + CHUNK], fetched, ALU.max)
            z_bf = sbuf(f"z_bf{c}", [P, CHUNK, PACK], BF16)
            nc.vector.tensor_tensor(words_by_line(z_bf[:]), planes_by_line(larger[:, c, :, :]), gt_by_line, ALU.mult)
            z_codes = sbuf(f"z_codes{c}", [P, CHUNK], U32)
            z_bytes = sbuf(f"z_bytes{c}", [P, CHUNK], U8)
            quantize(nc, z_codes[:], z_bytes[:], z_bf[:])
            z_parts.append((z_codes, z_bytes))

        h_banks = [psum.tile([P, H], F32, name=f"h_bank{t}", tag=f"bank{PACK + t}") for t in range(PACK)]
        for c, (z_codes, z_bytes) in enumerate(z_parts):
            for t in range(PACK):
                acc = h_banks[t][:, c * CHUNK : (c + 1) * CHUNK]
                product(nc, acc, w1_codes[:, blocks[t]], w1_bytes[:, blocks[t]], z_codes[:], z_bytes[:])

        w2_codes = sbuf("w2_codes", [P, N], U32)
        w2_bytes = sbuf("w2_bytes", [P, N], U8)
        w2_bf = sbuf("w2_bf", [P, N, PACK], BF16, reuses=last_y_n1)
        for cols in halves:
            nc.scalar.copy(words_by_line(w2_bf[:, cols, :]), planes_by_line(w2_raw[:, :, cols]))
            quantize(nc, w2_codes[:, cols], w2_bytes[:, cols], w2_bf[:, cols, :])

        gh = [sbuf(f"gh{t}", [P, H], F32) for t in range(PACK)]
        for t in range(PACK):
            nc.vector.tensor_scalar(gh[t][:], h_banks[t][:], gp_cols[:, t : t + 1], None, ALU.mult)

        out_rows = out.rearrange("(b p) j -> p b j", p=P)

        def finish(c, z2_codes, z2_bytes, row_blocks, bank, reuses=None):
            cols = slice(c * CHUNK, (c + 1) * CHUNK)
            count = row_blocks.stop - row_blocks.start
            acc = psum.tile([P, count, CHUNK], F32, name=f"out_bank{bank}", tag=f"bank{bank}")
            for b in range(count):
                rows = blocks[row_blocks.start + b]
                product(nc, acc[:, b, :], w2_codes[:, rows], w2_bytes[:, rows], z2_codes[:], z2_bytes[:])
            total = sbuf(f"total{bank}", [P, count, CHUNK], F32, reuses=reuses)
            nc.vector.tensor_tensor(total[:], acc[:], res_sb[:, row_blocks, cols], ALU.add)
            nc.sync.dma_start(out_rows[:, row_blocks, cols], total[:])

        fetched_first = sbuf("fetched_first", [P, 2, PACK, CHUNK], F32)
        fetched_rest = sbuf("fetched_rest", [P, CHUNKS - 1, 3, PACK, CHUNK], F32, reuses="gp_sb")
        z2_parts = []
        for c in range(CHUNKS):
            start = c * CHUNK
            fetched = fetched_first[:] if c == 0 else fetched_rest[:, c - 1, :, :, :]
            pa, gate = fetched[:, 0, :, :], fetched[:, 1, :, :]
            diff = sbuf(f"diff{c}", [P, PACK, CHUNK], F32)

            def fetch_gate(t):
                looked_up = gh[t][:].indirect(entries(n4_sb, start, CHUNK))
                nc.scalar.activation(gate[:, t, :], looked_up, ACT.Sigmoid, scale=undo_gp[:, t : t + 1])

            gates_ahead = 1 if c == 0 else 0
            for t in range(gates_ahead):
                fetch_gate(t)
            for t in range(PACK):
                fetch(pa[:, t, :], gh[t], n3_sb, start, CHUNK)
                if c >= SHARED_FROM and t == PACK - 1:
                    far = fetched[:, 2, t, :]
                    fetch(far, gh[t], n5_sb, start, CHUNK)
                else:
                    far = gh[t][:].indirect(entries(n5_sb, start, CHUNK))
                nc.vector.tensor_tensor(diff[:, t, :], far, pa[:, t, :], ALU.subtract)
            for t in range(gates_ahead, PACK):
                fetch_gate(t)
            step = sbuf(f"step{c}", [P, PACK, CHUNK], F32)
            for pair in (slice(0, 2), slice(2, 4)):
                nc.vector.tensor_tensor(step[:, pair, :], diff[:, pair, :], gate[:, pair, :], ALU.mult)
            z2_bf = sbuf(f"z2_bf{c}", [P, CHUNK, PACK], BF16)
            nc.vector.tensor_tensor(words_by_line(z2_bf[:]), planes_by_line(step[:]), planes_by_line(pa), ALU.add)
            z2_codes = sbuf(f"z2_codes{c}", [P, CHUNK], U32)
            z2_bytes = sbuf(f"z2_bytes{c}", [P, CHUNK], U8)
            quantize(nc, z2_codes[:], z2_bytes[:], z2_bf[:])
            z2_parts.append((z2_codes, z2_bytes))
            if c < CHUNKS - 2:
                finish(c, z2_codes, z2_bytes, slice(0, PACK), bank=c)

        last = CHUNKS - 1
        finish(last - 1, *z2_parts[last - 1], slice(0, PACK), bank=last - 1, reuses=f"z2_bf{last}")
        finish(last, *z2_parts[last], slice(0, 2), bank=last)
        finish(last, *z2_parts[last], slice(2, 4), bank=last + 1)
